import numpy as np
import ml_dtypes

BF16 = ml_dtypes.bfloat16


def bf(x):
    return np.asarray(x, np.float32).astype(BF16)


def f32(x):
    return np.asarray(x, np.float32)


def f64(x):
    return np.asarray(x).astype(np.float64)


def striped(idx):
    return np.tile(idx.reshape(-1, 16).T, (8, 1))


S, K, M, N, E, Q = 512, 128, 128, 128, 2, 64


def setup_inputs():
    return {"base": bf(np.random.standard_normal((M, S))), "x": bf(np.random.standard_normal((K, N))), "w": bf(np.random.standard_normal((E, K, M)) / np.sqrt(K)), "b": f32(0.5 * np.random.standard_normal((M, 1))), "offs": striped(np.random.permutation(S)[:N])}


def reference(base, x, w, b, offs):
    idx = offs[:16].T.reshape(-1)
    z = f64(base).copy()
    for e in range(E):
        z[:, idx[e * Q : (e + 1) * Q]] = f64(w)[e].T @ f64(x)[:, e * Q : (e + 1) * Q]
    return z + f64(b)

import concourse.mybir as mybir
from concourse.masks import make_identity

BF16, F32, U16 = mybir.dt.bfloat16, mybir.dt.float32, mybir.dt.uint16

S = 512
K = 128
M = 128
N = 128
E = 2
Q = N // E
COLS = Q // 16

FLOPS = 2 * M * K * N + M * S


def tile_scatter_matmul_kernel(tc, base, x, w, b, offs, out):
    nc = tc.nc
    with (
        tc.tile_pool(name="held", bufs=1) as held,
        tc.psum_pool(name="psum", bufs=1) as psum,
    ):
        base_tile = held.tile([M, S], BF16)
        offsets = held.tile([128, N // 16], U16)
        x_tile = held.tile([K, N], BF16)
        w_tile = held.tile([K, E, M], BF16)
        bias = held.tile([M, 1], F32)
        ident = held.tile([M, M], BF16)
        result = held.tile([M, S], F32)
        window = psum.tile([M, S], F32)

        nc.sync.dma_start(base_tile[:], base)
        nc.sync.dma_start(w_tile[:], w.rearrange("e k m -> k e m"))
        nc.sync.dma_start(x_tile[:], x)
        nc.sync.dma_start(offsets[:], offs)
        nc.sync.dma_start(bias[:], b)
        make_identity(nc, ident[:])

        nc.tensor.matmul(window[:], ident[:], base_tile[:], start=True, stop=True)

        for e in range(E):
            piece = offsets[:, e * COLS : (e + 1) * COLS]
            nc.tensor.matmul(
                window[:].indirect(piece),
                w_tile[:, e, :],
                x_tile[:, e * Q : (e + 1) * Q],
                start=True,
                stop=True,
            )

        nc.vector.tensor_scalar_add(result[:], window[:], bias[:, 0:1])
        nc.sync.dma_start(out, result[:])
